import numpy as np
import ml_dtypes


def mxq(x, axis, fmt="e4m3"):
    dtype, down = {"e4m3": (ml_dtypes.float8_e4m3fn, 7), "e5m2": (ml_dtypes.float8_e5m2, 14)}[fmt]
    v = np.moveaxis(np.asarray(x, np.float32).astype(ml_dtypes.bfloat16).astype(np.float64), axis, -1)
    blocks = v.reshape(v.shape[:-1] + (-1, 32))
    amax = np.abs(blocks).max(-1, keepdims=True)
    byte = np.maximum(np.where(amax > 0, np.frexp(amax)[1] - 1 + 127, 0) - down, 1)
    scale = np.exp2(byte - 127.0)
    codes = (blocks / scale).astype(np.float32).astype(dtype).astype(np.float64)
    return np.moveaxis((codes * scale).reshape(v.shape), -1, axis)


WIDE = False


def mx_kscale(k):
    if not WIDE:
        return np.ones(k)
    levels = np.array([10, -10, 5, -5, 0])
    if k % 512:
        return np.exp2(np.random.permutation(np.resize(levels, k // 32))).repeat(32)
    a = np.empty((k // 512, 16))
    for p in range(k // 512):
        a[p, :8] = np.random.permutation(np.resize(levels, 8))
        for g in range(8):
            far = levels[np.abs(levels - a[p, g]) >= 10]
            a[p, g + 8] = far[np.random.randint(len(far))]
    return np.exp2(a.ravel()).repeat(32)


def f64(x):
    return np.asarray(x).astype(np.float64)


def striped(idx):
    return np.tile(np.asarray(idx).reshape(-1, 16).T, (8, 1)).astype(np.uint16)


def unstriped(offs):
    return offs[:16].T.reshape(-1).astype(np.int64)


def striped8(idx):
    return np.asarray(idx).reshape(8, -1, 16).transpose(0, 2, 1).reshape(128, -1).astype(np.uint16)


def unstriped8(offs):
    return offs.reshape(8, 16, -1).transpose(0, 2, 1).reshape(8, -1).astype(np.int64)


def pick8(x, idx, run):
    r = np.arange(len(x))
    return x[r[:, None], idx[r % (8 * run) // run]]


E2M1 = np.array([0.0, 0.5, 1.0, 1.5, 2.0, 3.0, 4.0, 6.0, -0.0, -0.5, -1.0, -1.5, -2.0, -3.0, -4.0, -6.0])


def pack_weight(w, fmt):
    k, n = w.shape
    w = f64(np.asarray(w, np.float32).astype(ml_dtypes.bfloat16)).reshape(k // 32, 32, n)
    amax = np.abs(w).max(1)
    if fmt == "e4m3":
        byte = np.frexp(amax)[1] - 1 + 127 - 7
    else:
        mant, ex = np.frexp(amax / 6.0)
        byte = np.where(mant > 0.5, ex, ex - 1) + 127
    byte = np.clip(np.where(amax > 0, byte, 1), 1, 254)
    scaled = (w * np.exp2(127.0 - byte)[:, None, :]).reshape(k, n).astype(np.float32)
    by_word = np.ascontiguousarray(scaled.reshape(k // 512, 128, 4, n).transpose(0, 1, 3, 2))
    if fmt == "e4m3":
        words = by_word.astype(ml_dtypes.float8_e4m3fn).view(np.uint8)
    else:
        c = by_word.astype(ml_dtypes.float4_e2m1fn).view(np.uint8) & 0xF
        words = (c[..., 0::2] | (c[..., 1::2] << 4)).reshape(k // 512, 128, 2 * n)
    return np.ascontiguousarray(words), np.ascontiguousarray(byte.astype(np.uint8).reshape(k // 512, 16, n))


def unpack_weight(words, scales, fmt):
    g, _, n = scales.shape
    words = np.ascontiguousarray(words).reshape(g, 128, n, -1)
    if fmt == "e4m3":
        vals = words.view(ml_dtypes.float8_e4m3fn).astype(np.float64)
    else:
        nib = np.empty((g, 128, n, 4), np.uint8)
        nib[..., 0::2] = words & 0xF
        nib[..., 1::2] = words >> 4
        vals = E2M1[nib]
    vals = vals * np.repeat(np.exp2(scales.astype(np.float64) - 127.0), 8, axis=1)[..., None]
    return vals.transpose(0, 1, 3, 2).reshape(g * 512, n)


K, J, R, T, O, C, N, S, E = 512, 256, 512, 512, 128, 512, 256, 1024, 256


def setup_inputs():
    n = np.random.standard_normal
    idx = np.stack([np.random.permutation(T)[:J] for _ in range(8)])
    idx2 = np.stack([np.random.permutation(C)[:J] for _ in range(8)])
    idx3 = np.stack([np.random.permutation(C)[:O] for _ in range(8)])
    idx4 = np.stack([np.random.permutation(C)[:O] for _ in range(8)])
    idx5 = np.random.permutation(S)[:N]
    idx6 = np.stack([np.random.permutation(E)[:O] for _ in range(8)])
    idx7 = np.stack([np.random.permutation(E)[:O] for _ in range(8)])
    fk = mx_kscale(K)
    fr = mx_kscale(R)
    wp = pack_weight(n((K, R)) * 1 / np.sqrt(K) / fk[:, None] * fr, "e2m1")
    vsp = pack_weight(n((R, S)) * 1 / np.sqrt(R) / fr[:, None], "e4m3")
    return {
        "ta": (np.random.randint(-7, 8, (K, T)).astype(np.float64)).astype(np.float32),
        "ga": ((np.random.randint(8, 25, (K, 1)) / 64.0) * fk[:, None]).astype(np.float32),
        "w_words": wp[0],
        "w_scales": wp[1],
        "sa": (np.random.uniform(0.5, 1.6, (R, 1))).astype(np.float32),
        "sb": (np.random.uniform(0.5, 1.6, (R, 1))).astype(np.float32),
        "vs_words": vsp[0],
        "vs_scales": vsp[1],
        "tz": (np.random.randint(-7, 8, (N, E)).astype(np.float64)).astype(np.float32),
        "so": (np.random.randint(8, 25, (N, 1)) / 64.0).astype(np.float32),
        "sp": (np.random.randint(4, 15, (N, 1)) / 64.0).astype(np.float32),
        "offs": striped8(idx),
        "offs2": striped8(idx2),
        "offs3": striped8(idx3),
        "offs4": striped8(idx4),
        "offs5": striped(idx5),
        "offs6": striped8(idx6),
        "offs7": striped8(idx7),
    }


def reference(ta, ga, w_words, w_scales, sa, sb, vs_words, vs_scales, tz, so, sp, offs, offs2, offs3, offs4, offs5, offs6, offs7):
    idx = unstriped8(offs)
    idx2 = unstriped8(offs2)
    idx3 = unstriped8(offs3)
    idx4 = unstriped8(offs4)
    idx5 = unstriped(offs5)
    idx6 = unstriped8(offs6)
    idx7 = unstriped8(offs7)
    wu = unpack_weight(w_words, w_scales, "e2m1")
    vsu = unpack_weight(vs_words, vs_scales, "e4m3")
    xc = pick8(f64(ta), idx, 64) * f64(ga)
    xcq = mxq(xc, 0, "e4m3")
    a = wu.T @ xcq
    pw = np.zeros((R, C))
    pw[np.arange(R)[:, None], idx2[np.arange(R) % 512 // 64]] = a
    hid = np.abs(pick8(pw, idx3, 64) * f64(sa) - pick8(pw, idx4, 64) * f64(sb))
    vsidx5g = vsu[:, idx5]
    hidq = mxq(hid, 0, "e4m3")
    p = vsidx5g.T @ hidq
    y = np.maximum(np.minimum(p, pick8(f64(tz), idx6, 16) * f64(so)), pick8(f64(tz), idx7, 16) * f64(sp))
    return y

@@ -1,0 +1,183 @@
+from contextlib import ExitStack
+
+import concourse.mybir as mybir
+
+F32 = mybir.dt.float32
+BF16 = mybir.dt.bfloat16
+I32 = mybir.dt.int32
+U32 = mybir.dt.uint32
+U16 = mybir.dt.uint16
+U8 = mybir.dt.uint8
+FP8X4 = mybir.dt.float8_e4m3fn_x4
+FP4X4 = mybir.dt.float4_e2m1fn_x4
+ALU = mybir.AluOpType
+ACT = mybir.ActivationFunctionType
+
+P = 128
+K, J, R, T, O, C, N, S, E = 512, 256, 512, 512, 128, 512, 256, 1024, 256
+H = J // 2
+FLOPS = 2 * K * R * J + 2 * R * N * O
+
+
+def tile_picked_codes_plain_one_boardpair_store_lastbounds_kernel(
+    tc, ta, ga, w_words, w_scales, sa, sb, vs_words, vs_scales, tz, so, sp,
+    offs, offs2, offs3, offs4, offs5, offs6, offs7, out
+):
+    nc = tc.nc
+    with ExitStack() as ctx:
+        lists = ctx.enter_context(tc.tile_pool(name="lists", bufs=1))
+        keep = ctx.enter_context(tc.tile_pool(name="keep", bufs=1))
+        psum = ctx.enter_context(tc.psum_pool(name="psum", bufs=1))
+
+        def load_list(src, name):
+            t = lists.tile(list(src.shape), U16, name=name)
+            nc.sync.dma_start(t[:], src)
+            return t
+
+        def load_steps(src, name, queue):
+            t = keep.tile([P, 4], F32, name=name)
+            queue.dma_start(t[:], src.rearrange("(p t) o -> p (t o)", t=4))
+            return t
+
+        def load_scale_rows(plane, src, q, queue):
+            queue.dma_start(plane[32 * q : 32 * q + 4, :].bitcast(I32), src[0, 4 * q : 4 * q + 4, :].bitcast(I32))
+
+        w_plane = keep.tile([P, R], U8, name="w_plane", align_bytes=64)
+        vs_plane = keep.tile([P, S], U8, name="vs_plane", align_bytes=64)
+        nc.vector.memset(w_plane[:].bitcast(I32), 0)
+        nc.vector.memset(vs_plane[:].bitcast(I32), 0)
+
+        ta_rows = ta.rearrange("(p t) c -> p t c", t=4)
+        ta_sb = [keep.tile([P, T], F32, name="ta%d" % t) for t in range(4)]
+        nc.sync.dma_start(ta_sb[0][:], ta_rows[:, 0, :])
+        l1 = load_list(offs, "l1")
+        ga_sb = load_steps(ga, "ga_sb", nc.scalar)
+        w_stage = keep.tile([4, 4, R // 4], I32, name="w_stage")
+        nc.scalar.dma_start(w_stage[:], w_scales[0].bitcast(I32).rearrange("(q r) c -> r q c", q=4))
+        for t in range(1, 4):
+            nc.sync.dma_start(ta_sb[t][:], ta_rows[:, t, :])
+        w_raw = keep.tile([P, R], U16, name="w_raw", align_bytes=64)
+        nc.sync.dma_start(w_raw[:].bitcast(I32), w_words[0].bitcast(I32))
+        l2 = load_list(offs2, "l2")
+        tz_sb = [keep.tile([P, E], F32, name="tz%d" % b, align_bytes=64) for b in range(2)]
+        nc.sync.dma_start(tz_sb[0][:], tz[0:P, :])
+        l6 = load_list(offs6, "l6")
+        so_sb = keep.tile([P, 2], F32, name="so_sb")
+        sp_sb = keep.tile([P, 2], F32, name="sp_sb")
+        with nc.allow_non_contiguous_dma(reason="one value a partition and block"):
+            nc.sync.dma_start(so_sb[:], so.rearrange("(b p) o -> p (b o)", b=2))
+            l7 = load_list(offs7, "l7")
+            nc.sync.dma_start(sp_sb[:], sp.rearrange("(b p) o -> p (b o)", b=2))
+        nc.sync.dma_start(tz_sb[1][:], tz[P : 2 * P, :])
+        l3 = load_list(offs3, "l3")
+        sa_sb = load_steps(sa, "sa_sb", nc.sync)
+        l4 = load_list(offs4, "l4")
+        sb_sb = load_steps(sb, "sb_sb", nc.sync)
+        l5 = load_list(offs5, "l5")
+        vs_sb = keep.tile([P, S], I32, name="vs_sb")
+        nc.sync.dma_start(vs_sb[:], vs_words[0].rearrange("p c r -> p (c r)").bitcast(I32))
+        for q in range(4):
+            load_scale_rows(vs_plane, vs_scales, q, nc.sync)
+
+        board = [keep.tile([P, C], F32, name="board%d" % t, align_bytes=64) for t in range(4)]
+        for t in range(4):
+            nc.vector.memset(board[t][:], 0.0)
+
+        for q in range(4):
+            nc.vector.tensor_copy(w_plane[32 * q : 32 * q + 4, :].bitcast(I32), w_stage[:, q, :])
+        w_plane_d = keep.tile([P, R], U8, name="w_plane_d", align_bytes=64)
+        nc.vector.tensor_copy(
+            w_plane_d[:].rearrange("p (t m) -> p m t", t=4), w_plane[:].rearrange("p (m t) -> p m t", t=4)
+        )
+
+        xc01 = keep.tile([P, 2, J], BF16, name="xc01")
+        xc23 = keep.tile([P, 2, J], BF16, name="xc23")
+        xw = [keep.tile([P, H, 4], BF16, name="xw%d" % h, align_bytes=64) for h in range(2)]
+        for t in range(2):
+            nc.scalar.activation(xc01[:, t, :], ta_sb[t][:].indirect(l1[:]), ACT.Copy, scale=ga_sb[:, t : t + 1])
+        for h in range(2):
+            nc.vector.tensor_copy(xw[h][:, :, 0:2], xc01[:, :, H * h : H * (h + 1)].rearrange("p t j -> p j t"))
+        nc.scalar.activation(xc23[:, 0, :], ta_sb[2][:].indirect(l1[:]), ACT.Copy, scale=ga_sb[:, 2:3])
+        for h in range(2):
+            nc.scalar.activation(
+                xc23[:, 1, H * h : H * (h + 1)], ta_sb[3][:].indirect(l1[:, 8 * h : 8 * (h + 1)]), ACT.Copy,
+                scale=ga_sb[:, 3:4],
+            )
+
+        w_first = keep.tile([P, P], U16, name="w_first", align_bytes=64)
+        w_rest = keep.tile([P, 3, P], U16, name="w_rest", align_bytes=64)
+        w_by_t = w_raw[:].rearrange("p (m t) -> p m t", t=4)
+        nc.scalar.copy(w_first[:], w_by_t[:, :, 0])
+        nc.scalar.copy(w_rest[:].rearrange("p t m -> p m t"), w_by_t[:, :, 1:4])
+        w_d = [w_first[:]] + [w_rest[:, t, :] for t in range(3)]
+
+        x_codes = keep.tile([P, J], U32, name="x_codes", align_bytes=64)
+        x_plane = keep.tile([P, J], U8, name="x_plane", align_bytes=64)
+        for h in range(2):
+            nc.vector.tensor_copy(xw[h][:, :, 2:4], xc23[:, :, H * h : H * (h + 1)].rearrange("p t j -> p j t"))
+            nc.vector.quantize_mx(
+                x_codes[:, H * h : H * (h + 1)].bitcast(FP8X4), x_plane[:, H * h : H * (h + 1)],
+                xw[h][:].rearrange("p j t -> p (j t)"),
+            )
+
+        pieces = [(0, 0, H), (0, H, J), (1, 0, J), (2, 0, J), (3, 0, J)]
+        a_sb = {}
+
+        def product(i):
+            t, j0, j1 = pieces[i]
+            a_ps = psum.tile([P, j1 - j0], F32, name="a_ps%d" % i)
+            nc.tensor.matmul_mx(
+                a_ps[:], lhsT=w_d[t].bitcast(FP4X4), lhsT_scale=w_plane_d[:, P * t : P * (t + 1)],
+                rhs=x_codes[:, j0:j1].bitcast(FP8X4), rhs_scale=x_plane[:, j0:j1], start=True, stop=True,
+            )
+            a_t = keep.tile([P, j1 - j0], F32, name="a_sb%d" % i, tag=["a0", "a1", "a0", "tz0", "tz1"][i], align_bytes=64)
+            nc.scalar.copy(a_t[:], a_ps[:])
+            a_sb[i] = a_t
+
+        for i in range(2):
+            product(i)
+
+        hi = keep.tile([P, 2, O], F32, name="hi")
+        lo = keep.tile([P, 2, O], F32, name="lo")
+        diff = keep.tile([P, 3, O], F32, name="diff")
+        hid = keep.tile([P, O, 4], BF16, name="hid", align_bytes=64)
+        for i, (t, j0, j1) in enumerate(pieces):
+            nc.vector.tensor_copy(board[t][:].indirect(l2[:, j0 // 16 : j1 // 16]), a_sb[i][:])
+            if j1 < J:
+                product(2)
+                for b in range(2):
+                    nc.scalar.activation(hi[:, b, :], tz_sb[b][:].indirect(l6[:]), ACT.Copy, scale=so_sb[:, b : b + 1])
+                    nc.scalar.activation(lo[:, b, :], tz_sb[b][:].indirect(l7[:]), ACT.Copy, scale=sp_sb[:, b : b + 1])
+                    product(3 + b)
+                continue
+            g = keep.tile([P, 2, O], F32, name="g%d" % t, tag="board%d" % (t - 1) if t else "g0", align_bytes=64)
+            nc.scalar.activation(g[:, 0, :], board[t][:].indirect(l3[:]), ACT.Copy, scale=sa_sb[:, t : t + 1])
+            nc.scalar.activation(g[:, 1, :], board[t][:].indirect(l4[:]), ACT.Copy, scale=sb_sb[:, t : t + 1])
+            if t < 3:
+                nc.gpsimd.tensor_tensor(diff[:, t, :], g[:, 0, :], g[:, 1, :], ALU.subtract)
+
+        vs_g = keep.tile([P, N], U32, name="vs_g", tag="tz1", align_bytes=64)
+        nc.vector.tensor_copy(vs_g[:], vs_sb[:].bitcast(U32).indirect(l5[:]))
+        nc.scalar.activation(hid[:, :, 0:3], diff[:].rearrange("p t o -> p o t"), ACT.Abs)
+        diff_last = keep.tile([P, O], F32, name="diff_last", tag="vs_sb")
+        nc.vector.tensor_tensor(diff_last[:], g[:, 0, :], g[:, 1, :], ALU.subtract)
+        nc.scalar.activation(hid[:, :, 3], diff_last[:], ACT.Abs)
+
+        vs_plane_g = keep.tile([P, N], U8, name="vs_plane_g", tag="board2", align_bytes=64)
+        nc.vector.tensor_copy(vs_plane_g[:], vs_plane[:].indirect(l5[:]))
+
+        h_codes = keep.tile([P, O], U32, name="h_codes", tag="vs_plane", align_bytes=64)
+        h_plane = keep.tile([P, O], U8, name="h_plane", align_bytes=64)
+        nc.vector.quantize_mx(h_codes[:].bitcast(FP8X4), h_plane[:], hid[:].rearrange("p o t -> p (o t)"))
+
+        for b in range(2):
+            p_ps = psum.tile([P, O], F32, name="p_ps%d" % b)
+            nc.tensor.matmul_mx(
+                p_ps[:], lhsT=vs_g[:, P * b : P * (b + 1)].bitcast(FP8X4), lhsT_scale=vs_plane_g[:, P * b : P * (b + 1)],
+                rhs=h_codes[:].bitcast(FP8X4), rhs_scale=h_plane[:], start=True, stop=True,
+            )
+            capped = keep.tile([P, O], F32, name="capped%d" % b)
+            y = keep.tile([P, O], F32, name="y%d" % b)
+            nc.vector.tensor_tensor(capped[:], p_ps[:], hi[:, b, :], ALU.min)
+            nc.vector.tensor_tensor(y[:], capped[:], lo[:, b, :], ALU.max)
+            (nc.sync if b == 0 else nc.scalar).dma_start(out[P * b : P * (b + 1), :], y[:])

@@ -42,6 +42,9 @@ def tile_picked_codes_plain_one_boardpair_store_lastbounds_kernel(
         def load_scale_rows(plane, src, q, queue):
             queue.dma_start(plane[32 * q : 32 * q + 4, :].bitcast(I32), src[0, 4 * q : 4 * q + 4, :].bitcast(I32))
 
+        warm = keep.tile([P, 2], F32, name="warm")
+        nc.gpsimd.memset(warm[:], 0.0)
+        nc.scalar.activation(warm[:, 1:2], warm[:, 0:1], ACT.Abs)
         w_plane = keep.tile([P, R], U8, name="w_plane", align_bytes=64)
         vs_plane = keep.tile([P, S], U8, name="vs_plane", align_bytes=64)
         nc.vector.memset(w_plane[:].bitcast(I32), 0)

@@ -35,28 +35,32 @@ def tile_picked_codes_plain_one_boardpair_store_lastbounds_kernel(
             return t
 
         def load_steps(src, name, queue):
-            t = keep.tile([P, 4], F32, name=name)
+            t = keep.tile([P, 4], F32, name=name, align_bytes=64)
             queue.dma_start(t[:], src.rearrange("(p t) o -> p (t o)", t=4))
             return t
 
         def load_scale_rows(plane, src, q, queue):
             queue.dma_start(plane[32 * q : 32 * q + 4, :].bitcast(I32), src[0, 4 * q : 4 * q + 4, :].bitcast(I32))
 
+        w_plane = keep.tile([P, 2, R], U8, name="w_plane", align_bytes=64)
+        vs_plane = keep.tile([P, S], U8, name="vs_plane", align_bytes=64)
+        nc.gpsimd.memset(w_plane[:, 0, :].bitcast(I32), 0)
+        nc.vector.memset(vs_plane[:].bitcast(I32), 0)
+
         warm = keep.tile([P, 2], F32, name="warm")
         nc.gpsimd.memset(warm[:], 0.0)
         nc.scalar.activation(warm[:, 1:2], warm[:, 0:1], ACT.Abs)
-        w_plane = keep.tile([P, R], U8, name="w_plane", align_bytes=64)
-        vs_plane = keep.tile([P, S], U8, name="vs_plane", align_bytes=64)
-        nc.vector.memset(w_plane[:].bitcast(I32), 0)
-        nc.vector.memset(vs_plane[:].bitcast(I32), 0)
 
         ta_rows = ta.rearrange("(p t) c -> p t c", t=4)
         ta_sb = [keep.tile([P, T], F32, name="ta%d" % t) for t in range(4)]
         nc.sync.dma_start(ta_sb[0][:], ta_rows[:, 0, :])
         l1 = load_list(offs, "l1")
         ga_sb = load_steps(ga, "ga_sb", nc.scalar)
-        w_stage = keep.tile([4, 4, R // 4], I32, name="w_stage")
-        nc.scalar.dma_start(w_stage[:], w_scales[0].bitcast(I32).rearrange("(q r) c -> r q c", q=4))
+        for u in range(2):
+            nc.scalar.dma_start(
+                w_plane[64 * u : 64 * u + 4, :, :].bitcast(I32),
+                w_scales[0, 8 * u : 8 * u + 8, :].bitcast(I32).rearrange("(q r) c -> r q c", q=2),
+            )
         for t in range(1, 4):
             nc.sync.dma_start(ta_sb[t][:], ta_rows[:, t, :])
         w_raw = keep.tile([P, R], U16, name="w_raw", align_bytes=64)
@@ -72,38 +76,38 @@ def tile_picked_codes_plain_one_boardpair_store_lastbounds_kernel(
             l7 = load_list(offs7, "l7")
             nc.sync.dma_start(sp_sb[:], sp.rearrange("(b p) o -> p (b o)", b=2))
         nc.sync.dma_start(tz_sb[1][:], tz[P : 2 * P, :])
-        l3 = load_list(offs3, "l3")
-        sa_sb = load_steps(sa, "sa_sb", nc.sync)
-        l4 = load_list(offs4, "l4")
-        sb_sb = load_steps(sb, "sb_sb", nc.sync)
         l5 = load_list(offs5, "l5")
         vs_sb = keep.tile([P, S], I32, name="vs_sb")
         nc.sync.dma_start(vs_sb[:], vs_words[0].rearrange("p c r -> p (c r)").bitcast(I32))
         for q in range(4):
             load_scale_rows(vs_plane, vs_scales, q, nc.sync)
+        l3 = load_list(offs3, "l3")
+        sa_sb = load_steps(sa, "sa_sb", nc.sync)
+        l4 = load_list(offs4, "l4")
+        sb_sb = load_steps(sb, "sb_sb", nc.sync)
 
         board = [keep.tile([P, C], F32, name="board%d" % t, align_bytes=64) for t in range(4)]
         for t in range(4):
             nc.vector.memset(board[t][:], 0.0)
 
-        for q in range(4):
-            nc.vector.tensor_copy(w_plane[32 * q : 32 * q + 4, :].bitcast(I32), w_stage[:, q, :])
+        for u in range(2):
+            nc.vector.tensor_copy(
+                w_plane[64 * u + 32 : 64 * u + 36, 0, :].bitcast(I32), w_plane[64 * u : 64 * u + 4, 1, :].bitcast(I32)
+            )
         w_plane_d = keep.tile([P, R], U8, name="w_plane_d", align_bytes=64)
         nc.vector.tensor_copy(
-            w_plane_d[:].rearrange("p (t m) -> p m t", t=4), w_plane[:].rearrange("p (m t) -> p m t", t=4)
+            w_plane_d[:].rearrange("p (t m) -> p m t", t=4), w_plane[:, 0, :].rearrange("p (m t) -> p m t", t=4)
         )
 
-        xc01 = keep.tile([P, 2, J], BF16, name="xc01")
-        xc23 = keep.tile([P, 2, J], BF16, name="xc23")
-        xw = [keep.tile([P, H, 4], BF16, name="xw%d" % h, align_bytes=64) for h in range(2)]
-        for t in range(2):
-            nc.scalar.activation(xc01[:, t, :], ta_sb[t][:].indirect(l1[:]), ACT.Copy, scale=ga_sb[:, t : t + 1])
-        for h in range(2):
-            nc.vector.tensor_copy(xw[h][:, :, 0:2], xc01[:, :, H * h : H * (h + 1)].rearrange("p t j -> p j t"))
-        nc.scalar.activation(xc23[:, 0, :], ta_sb[2][:].indirect(l1[:]), ACT.Copy, scale=ga_sb[:, 2:3])
+        xc = keep.tile([P, 4, J], BF16, name="xc")
+        xw0 = keep.tile([P, H, 4], BF16, name="xw0", tag="xw", align_bytes=64)
+        for t in range(3):
+            nc.scalar.activation(xc[:, t, :], ta_sb[t][:].indirect(l1[:]), ACT.Copy, scale=ga_sb[:, t : t + 1])
+            if t == 1:
+                nc.vector.tensor_copy(xw0[:, :, 0:2], xc[:, 0:2, 0:H].rearrange("p t j -> p j t"))
         for h in range(2):
             nc.scalar.activation(
-                xc23[:, 1, H * h : H * (h + 1)], ta_sb[3][:].indirect(l1[:, 8 * h : 8 * (h + 1)]), ACT.Copy,
+                xc[:, 3, H * h : H * (h + 1)], ta_sb[3][:].indirect(l1[:, 8 * h : 8 * (h + 1)]), ACT.Copy,
                 scale=ga_sb[:, 3:4],
             )
 
@@ -114,25 +118,26 @@ def tile_picked_codes_plain_one_boardpair_store_lastbounds_kernel(
         nc.scalar.copy(w_rest[:].rearrange("p t m -> p m t"), w_by_t[:, :, 1:4])
         w_d = [w_first[:]] + [w_rest[:, t, :] for t in range(3)]
 
-        x_codes = keep.tile([P, J], U32, name="x_codes", align_bytes=64)
-        x_plane = keep.tile([P, J], U8, name="x_plane", align_bytes=64)
-        for h in range(2):
-            nc.vector.tensor_copy(xw[h][:, :, 2:4], xc23[:, :, H * h : H * (h + 1)].rearrange("p t j -> p j t"))
-            nc.vector.quantize_mx(
-                x_codes[:, H * h : H * (h + 1)].bitcast(FP8X4), x_plane[:, H * h : H * (h + 1)],
-                xw[h][:].rearrange("p j t -> p (j t)"),
-            )
+        x_codes = [keep.tile([P, H], U32, name="x_codes%d" % h, align_bytes=64) for h in range(2)]
+        x_plane = [keep.tile([P, H], U8, name="x_plane%d" % h, align_bytes=64) for h in range(2)]
+        nc.vector.tensor_copy(xw0[:, :, 2:4], xc[:, 2:4, 0:H].rearrange("p t j -> p j t"))
+        nc.vector.quantize_mx(x_codes[0][:].bitcast(FP8X4), x_plane[0][:], xw0[:].rearrange("p j t -> p (j t)"))
+        xw1 = keep.tile([P, H, 4], BF16, name="xw1", tag="xw", align_bytes=64)
+        nc.vector.tensor_copy(xw1[:], xc[:, :, H:J].rearrange("p t j -> p j t"))
+        nc.vector.quantize_mx(x_codes[1][:].bitcast(FP8X4), x_plane[1][:], xw1[:].rearrange("p j t -> p (j t)"))
 
-        pieces = [(0, 0, H), (0, H, J), (1, 0, J), (2, 0, J), (3, 0, J)]
+        pieces = [(0, 0, H), (1, 0, J), (0, H, J), (2, 0, J), (3, 0, J)]
         a_sb = {}
 
         def product(i):
             t, j0, j1 = pieces[i]
             a_ps = psum.tile([P, j1 - j0], F32, name="a_ps%d" % i)
-            nc.tensor.matmul_mx(
-                a_ps[:], lhsT=w_d[t].bitcast(FP4X4), lhsT_scale=w_plane_d[:, P * t : P * (t + 1)],
-                rhs=x_codes[:, j0:j1].bitcast(FP8X4), rhs_scale=x_plane[:, j0:j1], start=True, stop=True,
-            )
+            for j in range(j0, j1, H):
+                nc.tensor.matmul_mx(
+                    a_ps[:, j - j0 : j - j0 + H], lhsT=w_d[t].bitcast(FP4X4),
+                    lhsT_scale=w_plane_d[:, P * t : P * (t + 1)],
+                    rhs=x_codes[j // H][:].bitcast(FP8X4), rhs_scale=x_plane[j // H][:], start=True, stop=True,
+                )
             a_t = keep.tile([P, j1 - j0], F32, name="a_sb%d" % i, tag=["a0", "a1", "a0", "tz0", "tz1"][i], align_bytes=64)
             nc.scalar.copy(a_t[:], a_ps[:])
             a_sb[i] = a_t
@@ -142,34 +147,41 @@ def tile_picked_codes_plain_one_boardpair_store_lastbounds_kernel(
 
         hi = keep.tile([P, 2, O], F32, name="hi")
         lo = keep.tile([P, 2, O], F32, name="lo")
-        diff = keep.tile([P, 3, O], F32, name="diff")
-        hid = keep.tile([P, O, 4], BF16, name="hid", align_bytes=64)
-        for i, (t, j0, j1) in enumerate(pieces):
+        pairs = keep.tile([P, 2, 3, O], F32, name="pairs", align_bytes=64)
+        def scatter(i):
+            t, j0, j1 = pieces[i]
             nc.vector.tensor_copy(board[t][:].indirect(l2[:, j0 // 16 : j1 // 16]), a_sb[i][:])
-            if j1 < J:
-                product(2)
-                for b in range(2):
-                    nc.scalar.activation(hi[:, b, :], tz_sb[b][:].indirect(l6[:]), ACT.Copy, scale=so_sb[:, b : b + 1])
-                    nc.scalar.activation(lo[:, b, :], tz_sb[b][:].indirect(l7[:]), ACT.Copy, scale=sp_sb[:, b : b + 1])
-                    product(3 + b)
-                continue
-            g = keep.tile([P, 2, O], F32, name="g%d" % t, tag="board%d" % (t - 1) if t else "g0", align_bytes=64)
-            nc.scalar.activation(g[:, 0, :], board[t][:].indirect(l3[:]), ACT.Copy, scale=sa_sb[:, t : t + 1])
-            nc.scalar.activation(g[:, 1, :], board[t][:].indirect(l4[:]), ACT.Copy, scale=sb_sb[:, t : t + 1])
+
+        scatter(0)
+        product(2)
+        for b in range(2):
+            nc.scalar.activation(hi[:, b, :], tz_sb[b][:].indirect(l6[:]), ACT.Copy, scale=so_sb[:, b : b + 1])
+            nc.scalar.activation(lo[:, b, :], tz_sb[b][:].indirect(l7[:]), ACT.Copy, scale=sp_sb[:, b : b + 1])
+            product(3 + b)
+        for i in range(1, 5):
+            scatter(i)
+        for t in range(4):
             if t < 3:
-                nc.gpsimd.tensor_tensor(diff[:, t, :], g[:, 0, :], g[:, 1, :], ALU.subtract)
+                first, second = pairs[:, 0, t, :], pairs[:, 1, t, :]
+            else:
+                first = keep.tile([P, O], F32, name="first", tag="board1", align_bytes=64)[:]
+                second = keep.tile([P, O], F32, name="second", tag="board0", align_bytes=64)[:]
+            nc.scalar.activation(first, board[t][:].indirect(l3[:]), ACT.Copy, scale=sa_sb[:, t : t + 1])
+            nc.scalar.activation(second, board[t][:].indirect(l4[:]), ACT.Copy, scale=sb_sb[:, t : t + 1])
 
-        vs_g = keep.tile([P, N], U32, name="vs_g", tag="tz1", align_bytes=64)
+        diff = keep.tile([P, 3, O], F32, name="diff")
+        nc.vector.tensor_tensor(diff[:], pairs[:, 0, :, :], pairs[:, 1, :, :], ALU.subtract)
+        vs_g = keep.tile([P, N], U32, name="vs_g", tag="board2", align_bytes=64)
         nc.vector.tensor_copy(vs_g[:], vs_sb[:].bitcast(U32).indirect(l5[:]))
+        hid = keep.tile([P, O, 4], BF16, name="hid", tag="sb_sb", align_bytes=64)
         nc.scalar.activation(hid[:, :, 0:3], diff[:].rearrange("p t o -> p o t"), ACT.Abs)
-        diff_last = keep.tile([P, O], F32, name="diff_last", tag="vs_sb")
-        nc.vector.tensor_tensor(diff_last[:], g[:, 0, :], g[:, 1, :], ALU.subtract)
+        diff_last = keep.tile([P, O], F32, name="diff_last")
+        nc.vector.tensor_tensor(diff_last[:], first, second, ALU.subtract)
         nc.scalar.activation(hid[:, :, 3], diff_last[:], ACT.Abs)
-
-        vs_plane_g = keep.tile([P, N], U8, name="vs_plane_g", tag="board2", align_bytes=64)
+        vs_plane_g = keep.tile([P, N], U8, name="vs_plane_g", tag="board3", align_bytes=64)
         nc.vector.tensor_copy(vs_plane_g[:], vs_plane[:].indirect(l5[:]))
 
-        h_codes = keep.tile([P, O], U32, name="h_codes", tag="vs_plane", align_bytes=64)
+        h_codes = keep.tile([P, O], U32, name="h_codes", align_bytes=64)
         h_plane = keep.tile([P, O], U8, name="h_plane", align_bytes=64)
         nc.vector.quantize_mx(h_codes[:].bitcast(FP8X4), h_plane[:], hid[:].rearrange("p o t -> p (o t)"))
 

from contextlib import ExitStack

import concourse.mybir as mybir

F32 = mybir.dt.float32
BF16 = mybir.dt.bfloat16
I32 = mybir.dt.int32
U32 = mybir.dt.uint32
U16 = mybir.dt.uint16
U8 = mybir.dt.uint8
FP8X4 = mybir.dt.float8_e4m3fn_x4
FP4X4 = mybir.dt.float4_e2m1fn_x4
ALU = mybir.AluOpType
ACT = mybir.ActivationFunctionType

P = 128
K, J, R, T, O, C, N, S, E = 512, 256, 512, 512, 128, 512, 256, 1024, 256
H = J // 2
FLOPS = 2 * K * R * J + 2 * R * N * O


def tile_picked_codes_plain_one_boardpair_store_lastbounds_kernel(
    tc, ta, ga, w_words, w_scales, sa, sb, vs_words, vs_scales, tz, so, sp,
    offs, offs2, offs3, offs4, offs5, offs6, offs7, out
):
    nc = tc.nc
    with ExitStack() as ctx:
        lists = ctx.enter_context(tc.tile_pool(name="lists", bufs=1))
        keep = ctx.enter_context(tc.tile_pool(name="keep", bufs=1))
        psum = ctx.enter_context(tc.psum_pool(name="psum", bufs=1))

        def load_list(src, name):
            t = lists.tile(list(src.shape), U16, name=name)
            nc.sync.dma_start(t[:], src)
            return t

        def load_steps(src, name, queue):
            t = keep.tile([P, 4], F32, name=name, align_bytes=64)
            queue.dma_start(t[:], src.rearrange("(p t) o -> p (t o)", t=4))
            return t

        def load_scale_rows(plane, src, q, queue):
            queue.dma_start(plane[32 * q : 32 * q + 4, :].bitcast(I32), src[0, 4 * q : 4 * q + 4, :].bitcast(I32))

        w_plane = keep.tile([P, 2, R], U8, name="w_plane", align_bytes=64)
        vs_plane = keep.tile([P, S], U8, name="vs_plane", align_bytes=64)
        nc.gpsimd.memset(w_plane[:, 0, :].bitcast(I32), 0)
        nc.vector.memset(vs_plane[:].bitcast(I32), 0)

        warm = keep.tile([P, 2], F32, name="warm")
        nc.gpsimd.memset(warm[:], 0.0)
        nc.scalar.activation(warm[:, 1:2], warm[:, 0:1], ACT.Abs)

        ta_rows = ta.rearrange("(p t) c -> p t c", t=4)
        ta_sb = [keep.tile([P, T], F32, name="ta%d" % t) for t in range(4)]
        nc.sync.dma_start(ta_sb[0][:], ta_rows[:, 0, :])
        l1 = load_list(offs, "l1")
        ga_sb = load_steps(ga, "ga_sb", nc.scalar)
        for u in range(2):
            nc.scalar.dma_start(
                w_plane[64 * u : 64 * u + 4, :, :].bitcast(I32),
                w_scales[0, 8 * u : 8 * u + 8, :].bitcast(I32).rearrange("(q r) c -> r q c", q=2),
            )
        for t in range(1, 4):
            nc.sync.dma_start(ta_sb[t][:], ta_rows[:, t, :])
        w_raw = keep.tile([P, R], U16, name="w_raw", align_bytes=64)
        nc.sync.dma_start(w_raw[:].bitcast(I32), w_words[0].bitcast(I32))
        l2 = load_list(offs2, "l2")
        tz_sb = [keep.tile([P, E], F32, name="tz%d" % b, align_bytes=64) for b in range(2)]
        nc.sync.dma_start(tz_sb[0][:], tz[0:P, :])
        l6 = load_list(offs6, "l6")
        so_sb = keep.tile([P, 2], F32, name="so_sb")
        sp_sb = keep.tile([P, 2], F32, name="sp_sb")
        with nc.allow_non_contiguous_dma(reason="one value a partition and block"):
            nc.sync.dma_start(so_sb[:], so.rearrange("(b p) o -> p (b o)", b=2))
            l7 = load_list(offs7, "l7")
            nc.sync.dma_start(sp_sb[:], sp.rearrange("(b p) o -> p (b o)", b=2))
        nc.sync.dma_start(tz_sb[1][:], tz[P : 2 * P, :])
        l5 = load_list(offs5, "l5")
        vs_sb = keep.tile([P, S], I32, name="vs_sb")
        nc.sync.dma_start(vs_sb[:], vs_words[0].rearrange("p c r -> p (c r)").bitcast(I32))
        for q in range(4):
            load_scale_rows(vs_plane, vs_scales, q, nc.sync)
        l3 = load_list(offs3, "l3")
        sa_sb = load_steps(sa, "sa_sb", nc.sync)
        l4 = load_list(offs4, "l4")
        sb_sb = load_steps(sb, "sb_sb", nc.sync)

        board = [keep.tile([P, C], F32, name="board%d" % t, align_bytes=64) for t in range(4)]
        for t in range(4):
            nc.vector.memset(board[t][:], 0.0)

        for u in range(2):
            nc.vector.tensor_copy(
                w_plane[64 * u + 32 : 64 * u + 36, 0, :].bitcast(I32), w_plane[64 * u : 64 * u + 4, 1, :].bitcast(I32)
            )
        w_plane_d = keep.tile([P, R], U8, name="w_plane_d", align_bytes=64)
        nc.vector.tensor_copy(
            w_plane_d[:].rearrange("p (t m) -> p m t", t=4), w_plane[:, 0, :].rearrange("p (m t) -> p m t", t=4)
        )

        xc = keep.tile([P, 4, J], BF16, name="xc")
        xw0 = keep.tile([P, H, 4], BF16, name="xw0", tag="xw", align_bytes=64)
        for t in range(3):
            nc.scalar.activation(xc[:, t, :], ta_sb[t][:].indirect(l1[:]), ACT.Copy, scale=ga_sb[:, t : t + 1])
            if t == 1:
                nc.vector.tensor_copy(xw0[:, :, 0:2], xc[:, 0:2, 0:H].rearrange("p t j -> p j t"))
        for h in range(2):
            nc.scalar.activation(
                xc[:, 3, H * h : H * (h + 1)], ta_sb[3][:].indirect(l1[:, 8 * h : 8 * (h + 1)]), ACT.Copy,
                scale=ga_sb[:, 3:4],
            )

        w_first = keep.tile([P, P], U16, name="w_first", align_bytes=64)
        w_rest = keep.tile([P, 3, P], U16, name="w_rest", align_bytes=64)
        w_by_t = w_raw[:].rearrange("p (m t) -> p m t", t=4)
        nc.scalar.copy(w_first[:], w_by_t[:, :, 0])
        nc.scalar.copy(w_rest[:].rearrange("p t m -> p m t"), w_by_t[:, :, 1:4])
        w_d = [w_first[:]] + [w_rest[:, t, :] for t in range(3)]

        x_codes = [keep.tile([P, H], U32, name="x_codes%d" % h, align_bytes=64) for h in range(2)]
        x_plane = [keep.tile([P, H], U8, name="x_plane%d" % h, align_bytes=64) for h in range(2)]
        nc.vector.tensor_copy(xw0[:, :, 2:4], xc[:, 2:4, 0:H].rearrange("p t j -> p j t"))
        nc.vector.quantize_mx(x_codes[0][:].bitcast(FP8X4), x_plane[0][:], xw0[:].rearrange("p j t -> p (j t)"))
        xw1 = keep.tile([P, H, 4], BF16, name="xw1", tag="xw", align_bytes=64)
        nc.vector.tensor_copy(xw1[:], xc[:, :, H:J].rearrange("p t j -> p j t"))
        nc.vector.quantize_mx(x_codes[1][:].bitcast(FP8X4), x_plane[1][:], xw1[:].rearrange("p j t -> p (j t)"))

        pieces = [(0, 0, H), (1, 0, J), (0, H, J), (2, 0, J), (3, 0, J)]
        a_sb = {}

        def product(i):
            t, j0, j1 = pieces[i]
            a_ps = psum.tile([P, j1 - j0], F32, name="a_ps%d" % i)
            for j in range(j0, j1, H):
                nc.tensor.matmul_mx(
                    a_ps[:, j - j0 : j - j0 + H], lhsT=w_d[t].bitcast(FP4X4),
                    lhsT_scale=w_plane_d[:, P * t : P * (t + 1)],
                    rhs=x_codes[j // H][:].bitcast(FP8X4), rhs_scale=x_plane[j // H][:], start=True, stop=True,
                )
            a_t = keep.tile([P, j1 - j0], F32, name="a_sb%d" % i, tag=["a0", "a1", "a0", "tz0", "tz1"][i], align_bytes=64)
            nc.scalar.copy(a_t[:], a_ps[:])
            a_sb[i] = a_t

        for i in range(2):
            product(i)

        hi = keep.tile([P, 2, O], F32, name="hi")
        lo = keep.tile([P, 2, O], F32, name="lo")
        pairs = keep.tile([P, 2, 3, O], F32, name="pairs", align_bytes=64)
        def scatter(i):
            t, j0, j1 = pieces[i]
            nc.vector.tensor_copy(board[t][:].indirect(l2[:, j0 // 16 : j1 // 16]), a_sb[i][:])

        scatter(0)
        product(2)
        for b in range(2):
            nc.scalar.activation(hi[:, b, :], tz_sb[b][:].indirect(l6[:]), ACT.Copy, scale=so_sb[:, b : b + 1])
            nc.scalar.activation(lo[:, b, :], tz_sb[b][:].indirect(l7[:]), ACT.Copy, scale=sp_sb[:, b : b + 1])
            product(3 + b)
        for i in range(1, 5):
            scatter(i)
        for t in range(4):
            if t < 3:
                first, second = pairs[:, 0, t, :], pairs[:, 1, t, :]
            else:
                first = keep.tile([P, O], F32, name="first", tag="board1", align_bytes=64)[:]
                second = keep.tile([P, O], F32, name="second", tag="board0", align_bytes=64)[:]
            nc.scalar.activation(first, board[t][:].indirect(l3[:]), ACT.Copy, scale=sa_sb[:, t : t + 1])
            nc.scalar.activation(second, board[t][:].indirect(l4[:]), ACT.Copy, scale=sb_sb[:, t : t + 1])

        diff = keep.tile([P, 3, O], F32, name="diff")
        nc.vector.tensor_tensor(diff[:], pairs[:, 0, :, :], pairs[:, 1, :, :], ALU.subtract)
        vs_g = keep.tile([P, N], U32, name="vs_g", tag="board2", align_bytes=64)
        nc.vector.tensor_copy(vs_g[:], vs_sb[:].bitcast(U32).indirect(l5[:]))
        hid = keep.tile([P, O, 4], BF16, name="hid", tag="sb_sb", align_bytes=64)
        nc.scalar.activation(hid[:, :, 0:3], diff[:].rearrange("p t o -> p o t"), ACT.Abs)
        diff_last = keep.tile([P, O], F32, name="diff_last")
        nc.vector.tensor_tensor(diff_last[:], first, second, ALU.subtract)
        nc.scalar.activation(hid[:, :, 3], diff_last[:], ACT.Abs)
        vs_plane_g = keep.tile([P, N], U8, name="vs_plane_g", tag="board3", align_bytes=64)
        nc.vector.tensor_copy(vs_plane_g[:], vs_plane[:].indirect(l5[:]))

        h_codes = keep.tile([P, O], U32, name="h_codes", align_bytes=64)
        h_plane = keep.tile([P, O], U8, name="h_plane", align_bytes=64)
        nc.vector.quantize_mx(h_codes[:].bitcast(FP8X4), h_plane[:], hid[:].rearrange("p o t -> p (o t)"))

        for b in range(2):
            p_ps = psum.tile([P, O], F32, name="p_ps%d" % b)
            nc.tensor.matmul_mx(
                p_ps[:], lhsT=vs_g[:, P * b : P * (b + 1)].bitcast(FP8X4), lhsT_scale=vs_plane_g[:, P * b : P * (b + 1)],
                rhs=h_codes[:].bitcast(FP8X4), rhs_scale=h_plane[:], start=True, stop=True,
            )
            capped = keep.tile([P, O], F32, name="capped%d" % b)
            y = keep.tile([P, O], F32, name="y%d" % b)
            nc.vector.tensor_tensor(capped[:], p_ps[:], hi[:, b, :], ALU.min)
            nc.vector.tensor_tensor(y[:], capped[:], lo[:, b, :], ALU.max)
            (nc.sync if b == 0 else nc.scalar).dma_start(out[P * b : P * (b + 1), :], y[:])
